import numpy as np, ml_dtypes
CORES = [3,7,11,15,131,135,139,143]
N = 8
import mx_ref
BF = ml_dtypes.bfloat16
def gentries(a):
    return np.ascontiguousarray(a.reshape(8, 16, -1).transpose(0, 2, 1)).reshape(8, -1)
def gtable(e):
    e = np.asarray(e); return np.ascontiguousarray(e.reshape(8, -1, 16).transpose(0, 2, 1)).reshape(128, -1).astype(np.int32)
def gcols(t, e):
    v = np.concatenate([t.reshape(8, 16, -1, 4), np.zeros((8, 16, 1, 4), BF)], axis=2)
    return np.ascontiguousarray(np.stack([v[g][:, e[g]] for g in range(8)])).reshape(128, -1)
def gpick(z, e):
    return np.concatenate([z[16 * g:16 * g + 16][:, e[g]] for g in range(8)])
def tile(rs):
    return np.stack(rs, axis=2).reshape(128, -1).astype(BF)
def pick(q, e):
    c = np.concatenate([q[0].reshape(128, -1, 4), np.zeros((128, 1, 4), np.uint8)], axis=1); s = np.concatenate([q[1], np.ones((16, 1), np.uint8)], axis=1)
    return (np.ascontiguousarray(c[:, e].reshape(128, -1)), np.ascontiguousarray(s[:, e]))
def join(*qs):
    return (np.concatenate([q[0] for q in qs], axis=1), np.concatenate([q[1] for q in qs], axis=1))
def put(q, e, v):
    c, s = q[0].reshape(128, -1, 4).copy(), q[1].copy(); c[:, e] = v[0].reshape(128, -1, 4); s[:, e] = v[1]
    return (c.reshape(128, -1), s)
def pk(c, s):
    return (np.ascontiguousarray(c), mx_ref.live(s))
def emit(q):
    return q[0], q[1]
def packed(v, rng):
    q = [mx_ref.quantize(np.ascontiguousarray(v[r])) for r in range(N)]
    return np.stack([a for a, b in q]), np.stack([mx_ref.plane(b, rng) for a, b in q])
def values_of_codes():
    e, c = np.zeros((128, 128, 4), np.float32), np.zeros((128, 2, 4), np.uint8)
    e[np.arange(128), np.arange(128), 0] = 1
    c[:127, :, 0] = np.arange(256).reshape(2, 128).T[:127]
    return mx_ref.matmul(mx_ref.quantize(e.reshape(128, 512).astype(BF)), (c.reshape(128, 8), np.full((16, 2), 127, np.uint8))).T.reshape(-1).astype(np.float64)
CODE_VALUE, SCALE_VALUE = values_of_codes(), 2.0 ** (np.arange(256) - 127.0)
def decode(q):
    return (CODE_VALUE[q[0]].reshape(16, 8, -1, 4) * SCALE_VALUE[q[1]][:, None, :, None] + 0.0).reshape(128, -1).astype(np.float32)
def f(rng, *shape):
    return mx_ref.flush((rng.standard_normal(shape, dtype=np.float32) * np.exp2(rng.integers(-2, 3, shape[:-1] + (1,)))).astype(BF))
def wide(rng, *shape, cols=0):
    v = rng.standard_normal(shape, dtype=np.float32) * np.exp2(rng.integers(-12, 13, shape)).astype(np.float32)
    if cols: v *= np.repeat(np.exp2(rng.integers(-cols, cols + 1, shape[:-2] + (1, shape[-1] // 4))) * (rng.random(shape[:-2] + (1, shape[-1] // 4)) > 0.0625), 4, axis=-1).astype(np.float32)
    return mx_ref.flush(v.astype(BF))
C = 320
MASK = [1, 2, 4]
PARITY = np.array([(r ^ (r >> 1) ^ (r >> 2)) & 1 for r in range(N)])
def numbers_of(rng):
    return {"x": np.array(f(rng, N, 128, 4 * C)), "u": np.array(f(rng, N, 128, 512)), "v": np.array(f(rng, N, 128, 512))}
def stored(k):
    return {"fl": np.stack([gtable(k[r]) for r in range(N)])}
def lists(rng):
    return stored(rng.permuted(np.tile(np.arange(C), (N, 8, 1)), axis=2))
def layers(rng):
    return np.array(f(rng, N, 128, 2048)).reshape(N, 8, 16, 4, 8, 16, 4)
def weights(rng, w):
    c, p = packed(np.ascontiguousarray(w).reshape(N, 128, 2048), rng)
    return {"wc": c, "ws": p}
def setup_inputs(rng):
    return {**numbers_of(rng), **lists(rng), **weights(rng, layers(rng))}
def setup_inputs_long(rng):
    d = numbers_of(rng)
    kind = rng.permutation(8)
    s = np.tile(rng.choice([-1.0, 1.0], (8, C)), (N, 1, 1))
    k = np.zeros((N, 8, C), np.int64)
    for g in range(8):
        c, p = rng.permutation(C), int(rng.integers(C))
        if kind[g] == 0: c, p = np.arange(C), C - N // 2
        if kind[g] == 1: c = np.arange(C)[::-1]
        k[:, g, c] = np.roll(c, -1)
        for r in range(N):
            if kind[g] in (0, 1, 3, 4): s[r, g, c[(p + r) % C]] *= -1
            if kind[g] == 2 and PARITY[r]: s[r, g, c[p]] *= -1
            if kind[g] == 6 and PARITY[r]: s[r, g] *= -1
            if kind[g] == 7:
                s[r, g] = rng.choice([-1.0, 1.0], C)
                k[r, g] = np.arange(C)
    x = d["x"].reshape(N, 8, 16, C, 4)
    x[:, :, 0] = 0
    x[:, :, 0, :, 0] = s.astype(np.float32).astype(BF)
    u = d["u"].reshape(N, 128, 128, 4)
    u[:, :, ::16] = 0
    for h in range(0, 128, 16): u[:, h, h, 0] = 1
    w = layers(rng)
    w[:, :, :, :, :, 0] = 0
    return {"x": x.reshape(N, 128, 4 * C), "u": u.reshape(N, 128, 512), "v": d["v"], **stored(k), **weights(rng, w)}
def setup_inputs_near(rng):
    d = numbers_of(rng)
    o, e = rng.permutation(N) % 2, rng.permutation(N)
    k = np.where(o == 0, 2.0 ** -27, 1.0)
    m = np.where(o == 0, 2.0 ** -30, 1.0)
    s = rng.integers(-1, 2, (N, 8, C))
    s[e[0]] = 0
    s[e[1]] = 1
    x = d["x"].astype(np.float32).reshape(N, 8, 16, C, 4)
    x[o == 0] = 0
    x[:, :, :3] = 0
    x[:, :, 8:] = 0
    x[:, :, 0, :, 0] = np.where(s == 0, 1.0, 1.125 * s) * k[:, None, None]
    x[:, :, 1, :, 0] = np.where(s == 0, -1.125, -1.25 * s) * k[:, None, None]
    x[:, :, 3, :, 0] = k[:, None, None]
    x[:, :, 8, :, 0] = rng.choice([-1.0, 1.0], (N, 8, C)) * 2.0 ** -30
    x[:, :, 9, :, 0] = 2.0 ** -26
    for r in range(N):
        for g in rng.permutation(8)[:4]: x[r, g, 0, rng.integers(C), 0] = 2.0 ** 30 * rng.choice([-1.0, 1.0])
    u = d["u"].reshape(N, 128, 128, 4)
    u[:, :, ::16] = 0
    for h in range(0, 128, 16):
        u[:, h, h, 0] = (1.125 * m).astype(np.float32).astype(BF)
        u[:, h + 1, h, 0] = m.astype(np.float32).astype(BF)
        u[:, h + 2, h, 0] = m.astype(np.float32).astype(BF)
    w = layers(rng)
    w[:, :, :, :, :, :10] = 0
    for g in range(8): w[:, g, 8, 0, g, 2, 0] = 2.0 ** -7
    return {"x": x.reshape(N, 128, 4 * C).astype(BF), "u": u.reshape(N, 128, 512), "v": d["v"], **lists(rng), **weights(rng, w)}
def setup_inputs_odd(rng):
    d = numbers_of(rng)
    e = (PARITY[:, None] + rng.permutation(8)) % 2
    a = 1.0 + (2 * rng.integers(0, 64, (N, 8, 16, C, 4)) + 1) * 2.0 ** -7
    x = np.zeros((N, 8, 16, C, 4))
    x[:, :, :8] = a[:, :, :8] * np.exp2(-rng.integers(0, 7, (N, 8, 8, C, 4)).astype(np.float64)) * rng.choice([-1.0, 1.0], (N, 8, 8, C, 4))
    x[:, :, 0] = 0
    x[:, :, 0, :, 0] = 1.96875 * 2.0 ** 8 * rng.choice([-1.0, 1.0], (N, 8, C))
    x[:, :, 8:] = np.where(e[:, :, None, None, None] == 0, a[:, :, 8:] * np.exp2(12.0 - rng.integers(8, 15, (N, 8, 8, C, 4))), 0.0)
    x[:, :, 8, :, 0] = (np.where(e == 0, -1.0, 1.0) * 1.96875 * 2.0 ** 12)[:, :, None]
    u = d["u"].reshape(N, 128, 128, 4)
    u[:, 8::16, ::16] = 0
    w = layers(rng)
    for i in (0, 8):
        w[:, :, i] = 0
        w[:, :, :, :, :, i] = 0
    for g in rng.permutation(8)[:4]:
        x[:, g, :3] = 0
        x[:, g, 0, :, 0] = 1.96875 * 2.0 ** 8
        x[:, g, 1, :, 0] = (8 + rng.integers(-1, 2, (N, C))) * 2.0 ** -8
        x[:, g, 2, :, 0] = -2.0 ** -5
        x[:, g, 8:] = 0
        x[:, g, 8, :, 0] = 1.96875 * 2.0 ** 12
        x[:, g, 9] = rng.integers(1, 16, (N, C, 4)) * 2.0 ** -4
        u[:, 16 * g, ::16] = 0
        u[:, :, 16 * g] = 0
        u[:, 16 * g + 1:16 * g + 3, 16 * g, 0] = 1
        w[:, :, :, :, g] = 0
        for i in (0, 8): w[:, g, i, 0, g, i, 0] = -0.5
        for b in range(4): w[:, g, 9, b, g, 10, b] = 256.0
    return {"x": x.astype(np.float32).reshape(N, 128, 4 * C).astype(BF), "u": u.reshape(N, 128, 512), "v": d["v"], **lists(rng), **weights(rng, w)}
def setup_inputs_ends(rng):
    d = numbers_of(rng)
    x = np.zeros((N, 8, 16, C, 4))
    u = d["u"].astype(np.float32).reshape(N, 128, 128, 4)
    v = np.zeros((N, 128, 512))
    w = np.zeros((N, 128, 4, 128, 4), np.float32)
    o = rng.permutation(N) % 4
    third, others = np.flatnonzero(o == 2), np.flatnonzero(o != 2)
    if len(third) == 2 and third[0] ^ third[1] == MASK[0]:
        p = rng.choice(others)
        o[third[1]] = o[p]
        o[p] = 2
    i, at = np.arange(128), np.arange(C)
    k = np.zeros((N, 8, C), np.int64)
    for r in range(N):
        h = rng.permutation(8)
        c = np.where(h < 2, 0.0, h % 2 * 2.0 - 1.0)[None, :, None]
        low = -(0.9 + 0.1 * rng.random((8, 16, C, 4))) * 2.0 ** 30
        if o[r] == 0: x[r] = low
        if o[r] == 1: x[r] = low * rng.choice([-1.0, 1.0], C)[:, None]
        if o[r] == 2: x[r] = -(1.0 + 0.125 * rng.integers(0, 8, (8, 16, C, 4))) * 2.0 ** -30
        if o[r] == 3: x[r] = d["x"][r].astype(np.float32).reshape(8, 16, C, 4)[:, :, :1]
        if o[r] < 2:
            u[r, :, ::16] = c * (0.9 + 0.1 * rng.random((128, 8, 4))) * 2.0 ** 30
            v[r] = rng.choice([-1.0, 1.0], (128, 512)) * (0.9 + 0.1 * rng.random((128, 512))) * 2.0 ** 30
        else: v[r] = rng.choice([-1.0, 1.0], (128, 512)) * (1.0 + 0.125 * rng.integers(0, 8, (128, 512))) * 2.0 ** -30
        if o[r] == 2: u[r, :, ::16] = c * (1.0 + 0.125 * rng.integers(0, 8, (128, 8, 4))) * 2.0 ** -30
        if o[r] == 3: u[r, :, ::16] *= np.abs(c).astype(np.float32)
        t = np.array([4.0, 8.0, 16.0])[rng.permutation(8) % 3]
        if o[r] == 2: t[:] = 2.0 ** -8
        if o[r] == 3: t[:] = 2.0 ** 5
        for b in range(4): w[r, i, b, i, b] = t[i // 16]
        for g, n in enumerate(rng.permutation(8) % 5): k[r, g] = [at, at[::-1], np.roll(at, -1), at ^ 1, rng.permutation(C)][n]
    return {"x": x.astype(np.float32).reshape(N, 128, 4 * C).astype(BF), "u": u.reshape(N, 128, 512).astype(BF), "v": v.astype(np.float32).astype(BF), **stored(k), **weights(rng, w.astype(BF))}
def setup_inputs_spread(rng):
    d = numbers_of(rng)
    w = layers(rng).reshape(N, 128, 4, 128, 4)
    i, r = np.arange(128), int(rng.integers(N))
    for b in range(4): w[r, i, b, i, b] = 256.0
    return {"x": wide(rng, N, 128, 4 * C, cols=6), "u": d["u"], "v": d["v"], **lists(rng), **weights(rng, w)}
def check_inputs(d):
    b = []
    for k in ("x", "u", "v"):
        a = np.abs(d[k].astype(np.float32))
        if not (np.isfinite(a).all() and ((a == 0) | (a >= 2.0 ** -30) & (a <= 2.0 ** 30)).all()): b.append("a value of " + k)
    none, least, most = [emit(mx_ref.quantize(np.full((128, 16), k, np.float32).astype(BF)))[1][0, 0] for k in (0.0, 2.0 ** -8, 2.0 ** 8)]
    for r in range(N):
        if not (np.sort(gentries(d["fl"][r]), axis=1) == np.arange(C)).all(): b.append("fl: a group's entries are no permutation")
        if ((d["wc"][r] == 0x7F) | (d["wc"][r] == 0xFF)).any(): b.append("wc: a code that is no number")
        s = mx_ref.live(d["ws"][r])
        if ((s != none) & ((s < least) | (s > most))).any(): b.append("ws: a scale out of range")
        if (((d["wc"][r].reshape(16, 8, 512, 4) & 0x7F) != 0) & (s == none)[:, None, :, None]).any(): b.append("wc: a code other than zero under the scale of zeros")
    return b
def returns(e, gate):
    at = np.tile(np.arange(C), (8, 1))
    step = np.where(gate, at, e)
    a = e
    for i in range(C): a = np.take_along_axis(step, a, axis=1)
    return np.where(gate, a, at)
def reference(x, u, v, fl, wc, ws):
    half = np.float32(0.5)
    qu = [mx_ref.quantize(u[r]) for r in range(N)]
    lay = [pk(wc[r], ws[r]) for r in range(N)]
    own = [gentries(fl[r]).astype(np.int64) for r in range(N)]
    now = [x[r] for r in range(N)]
    for m in MASK:
        q = [mx_ref.quantize(now[r]) for r in range(N)]
        t = [decode(q[r]) for r in range(N)]
        bit = [mx_ref.matmul(qu[r], q[r])[::16] > 0 for r in range(N)]
        made, new = [], []
        for r in range(N):
            d = r ^ m
            a = returns(own[d], bit[r] != bit[d])
            n = np.take_along_axis(own[r], a, axis=1)
            z = (gcols(t[r].astype(BF), n).astype(np.float32) + gcols(t[d].astype(BF), a).astype(np.float32)) * half
            qz = mx_ref.quantize(z.astype(BF))
            back = np.argsort(n, axis=1)
            p = [mx_ref.matmul(pick(lay[r], np.arange(128 * b, 128 * b + 128)), qz) * np.float32(0.03125) for b in range(4)]
            made.append(tile([(t[r][:, b::4] + gpick(p[b], back)) * half for b in range(4)]))
            new.append(n)
        now, own = made, new
    y, ln = np.zeros((N, 128, C), np.float32), np.zeros((N, 8, C), np.float32)
    oc, osc = np.zeros((N, 128, 4 * C), np.uint8), np.zeros((N, 16, C), np.uint8)
    for r in range(N):
        q = mx_ref.quantize(now[r])
        y[r] = mx_ref.matmul(mx_ref.quantize(v[r]), q)
        ln[r] = own[r]
        oc[r], osc[r] = emit(q)
    return {"y": y, "ln": ln, "oc": oc, "osc": osc}

@@ -1,0 +1,347 @@
+from concourse.mybir import dt, AluOpType, ActivationFunctionType
+
+C = 320
+MASK = [1, 2, 4]
+SCHED = [2, 2, 2, 1, 1, 1]
+NW = 1 + sum(SCHED)
+FW2W = 1056
+
+SCRATCH = {
+    "I1": ("sbuf", [128, C], "int32"), "IB": ("sbuf", [128, C], "int32"),
+    "IOS": ("sbuf", [128, C], "bfloat16"), "MSK": ("sbuf", [128, C], "bfloat16"), "NMS": ("sbuf", [128, C], "bfloat16"),
+    "OI": ("sbuf", [128, 8], "int32"), "UO": ("sbuf", [128, 8], "uint16"),
+    "ATS": ("sbuf", [128, 20], "float32"),
+    "ET": ("sbuf", [128, 2048], "bfloat16"),
+    "EQ": ("sbuf", [128, 512], "float8_e4m3fn_x4"), "ES": ("sbuf", [128, 512], "uint8"),
+    "UT": ("sbuf", [128, 512], "bfloat16"), "VT": ("sbuf", [128, 512], "bfloat16"),
+    "UQ": ("sbuf", [128, 128], "float8_e4m3fn_x4"), "US": ("sbuf", [128, 128], "uint8"),
+    "UQ2": ("sbuf", [128, 128], "float8_e4m3fn_x4"), "US2": ("sbuf", [128, 128], "uint8"),
+    "VQ": ("sbuf", [128, 128], "float8_e4m3fn_x4"), "VS": ("sbuf", [128, 128], "uint8"),
+    "WQ": ("sbuf", [128, 512], "float8_e4m3fn_x4"), "WS": ("sbuf", [128, 512], "uint8"),
+    "FLI": ("sbuf", [128, 20], "int32"),
+    "AI3": ("sbuf", [128, C], "bfloat16"),
+    "FW1": ("sbuf", [128, 640], "bfloat16"), "FW2": ("sbuf", [128, FW2W], "bfloat16"),
+    "MK": ("sbuf", [128, C], "bfloat16"), "SC": ("sbuf", [128, C], "bfloat16"),
+    "LNF": ("sbuf", [128, C], "float32"), "YS": ("sbuf", [128, C], "float32"),
+    "PS": ("psum", [128, 4096], "float32"),
+}
+for _r in range(4):
+    SCRATCH.update({
+        "X%d" % _r: ("sbuf", [128, 4 * C], "bfloat16"),
+        "QX%d" % _r: ("sbuf", [128, C], "float8_e4m3fn_x4"), "SX%d" % _r: ("sbuf", [128, C], "uint8"),
+        "FS%d" % _r: ("sbuf", [128, C], "bfloat16"),
+        "FT%d" % _r: ("sbuf", [128, 20], "uint16"), "FI%d" % _r: ("sbuf", [128, 20], "uint16"),
+        "F4%d" % _r: ("sbuf", [128, 80], "uint16"),
+        "PK%d" % _r: ("sbuf", [128, 40], "bfloat16"),
+    })
+for _r in range(3):
+    SCRATCH.update({
+        "LP%d" % _r: ("sbuf", [128, 40], "bfloat16"),
+        "LQ%d" % _r: ("sbuf", [128, C], "float8_e4m3fn_x4"), "LS%d" % _r: ("sbuf", [128, C], "uint8"),
+        "XF%d" % _r: ("sbuf", [128, 4 * C], "bfloat16"),
+        "QF%d" % _r: ("sbuf", [128, C], "float8_e4m3fn_x4"), "SF%d" % _r: ("sbuf", [128, C], "uint8"),
+        "F%d" % _r: ("sbuf", [128, 4 * C], "bfloat16"), "M%d" % _r: ("sbuf", [128, 4 * C], "bfloat16"),
+        "Z%d" % _r: ("sbuf", [128, 4 * C], "bfloat16"),
+        "QZ%d" % _r: ("sbuf", [128, C], "float8_e4m3fn_x4"), "SZ%d" % _r: ("sbuf", [128, C], "uint8"),
+        "PW%d" % _r: ("sbuf", [128, 4 * C], "float32"),
+        "WN%d" % _r: ("sbuf", [128, C * NW], "bfloat16"),
+        "TB%d" % _r: ("sbuf", [128, 20 * 12], "uint16"), "TF%d" % _r: ("sbuf", [128, 20 * 10], "float32"),
+        "AT%d" % _r: ("sbuf", [128, 20], "uint16"), "AI%d" % _r: ("sbuf", [128, C], "bfloat16"),
+    })
+SEMAPHORES = ["sV", "sS", "sP", "sG", "lsent"] + ["d%d" % i for i in range(16)] + [k + str(r) for r in range(3) for k in ("apk", "aq", "asc")]
+
+
+def rank_program(g, core, T, topo):
+    rank = T.rank_of(core)
+    if rank is None:
+        return
+    A = AluOpType
+    COPY = ActivationFunctionType.Copy
+    v, s, pe = g.vector, g.scalar, g.tensor
+    queue = {"V": v, "S": s, "P": pe, "G": g, "Y": g.sync}
+
+    count = {}
+    known = {q: {} for q in queue}
+    behind = {}
+    writers, readers = {}, {}
+
+    def reg(name, lo=0, hi=None, lane=None):
+        return (name, lo, T[name].shape[1] if hi is None else hi, lane)
+
+    def meet(a, b):
+        return a[1] < b[2] and b[1] < a[2] and (a[3] is None or b[3] is None or a[3] == b[3])
+
+    def need(q, toks):
+        best = {}
+        for (sem, val) in toks:
+            if known[q].get(sem, 0) < val and best.get(sem, 0) < val:
+                best[sem] = val
+        for sem in list(best):
+            for sem2, val2 in best.items():
+                if sem2 != sem and behind.get((sem2, val2), {}).get(sem, 0) >= best[sem]:
+                    best[sem] = 0
+                    break
+        for sem, val in best.items():
+            if val:
+                queue[q].wait_ge(T.sem[sem], val)
+                known[q][sem] = max(val, known[q].get(sem, 0))
+                for k2, v2 in behind.get((sem, val), {}).items():
+                    known[q][k2] = max(v2, known[q].get(k2, 0))
+
+    def deps(q, rd, wr, dma):
+        toks = []
+        for r_ in rd:
+            toks += [t for (x, t, e) in writers.get(r_[0], []) if meet(x, r_)]
+        for w_ in wr:
+            toks += [t for (x, t, e) in writers.get(w_[0], []) if meet(x, w_) and not (q == "P" and e == q)]
+            toks += [t for (x, t, e) in readers.get(w_[0], []) if meet(x, w_) and (dma or e != q)]
+        need(q, toks)
+
+    def note(q, rd, wr, tok, e):
+        behind[tok] = dict(known[q])
+        for r_ in rd:
+            readers.setdefault(r_[0], []).append((r_, tok, e))
+        for w_ in wr:
+            writers.setdefault(w_[0], []).append((w_, tok, e))
+
+    def op(q, call, rd, wr):
+        deps(q, rd, wr, False)
+        sem = "s" + q
+        count[sem] = count.get(sem, 0) + 1
+        call().then_inc(T.sem[sem], 1)
+        note(q, rd, wr, (sem, count[sem]), q)
+
+    ndma = [0]
+
+    def dma(q, out, in_, rd, wr):
+        deps(q, rd, wr, True)
+        sem = "d%d" % ndma[0]
+        ndma[0] += 1
+        count[sem] = 16
+        queue[q].dma_start(out, in_).then_inc(T.sem[sem], 16)
+        note(q, rd, wr, (sem, 16), "dma" + sem)
+
+    def send(dst, out, in_, rd, land, sem):
+        deps("G", rd, [], True)
+        rid, pid = topo.addr(dst, core)
+        mask = topo.mask(core, dst)
+        n = len(topo.engines(core, dst))
+        g.remote_dma(out, in_, T.sem[sem], T.sem["lsent"], pid, rid, mask)
+        count["lsent"] = count.get("lsent", 0) + n
+        arrives = len(topo.engines(dst, core))
+        count[sem] = arrives
+        behind[(sem, arrives)] = {}
+        writers.setdefault(land[0], []).append((land, (sem, arrives), "far"))
+
+    def u8(ap):
+        return ap.bitcast(dt.uint8)
+
+    def u32(ap):
+        return ap.bitcast(dt.uint32)
+
+    def gather_masked(win, winreg, tab, tabreg):
+        op("V", lambda: v.tensor_tensor(T.MK[:], win.indirect(tab), T.MSK[:], A.mult), [winreg, tabreg, reg("MSK")], [reg("MK")])
+
+    def scan():
+        op("V", lambda: v.tensor_tensor_scan(T.SC[:], T.NMS[:], T.MK[:], 0.0, A.mult, A.add), [reg("MK"), reg("NMS")], [reg("SC")])
+
+    def sample(out, outreg, mul, add):
+        if mul == 1.0 and add == 0.0:
+            op("V", lambda: v.tensor_copy(out, T.SC[:, 15:C:16]), [reg("SC")], [outreg])
+        elif mul == 1.0:
+            op("V", lambda: v.tensor_scalar(out, T.SC[:, 15:C:16], add, None, A.add), [reg("SC")], [outreg])
+        else:
+            op("V", lambda: v.tensor_scalar(out, T.SC[:, 15:C:16], mul, add, A.mult, A.add), [reg("SC")], [outreg])
+
+    def gather_s(out, outreg, win, winreg, tab, tabreg):
+        op("S", lambda: s.activation(out, win.indirect(tab), COPY), [winreg, tabreg], [outreg])
+
+    def mm(bank, lq, ls, lo, rq, rs, start=True, stop=True):
+        b0 = 512 * bank
+        op("P", lambda: pe.matmul_mx(T.PS[:, b0:b0 + C], T[lq][:, lo:lo + 128], T[ls][:, lo:lo + 128], T[rq][:], T[rs][:], start, stop),
+           [reg(lq, lo, lo + 128), reg(ls, lo, lo + 128), reg(rq), reg(rs)], [reg("PS", b0, b0 + 512)])
+
+    def bank(b):
+        return reg("PS", 512 * b, 512 * b + 512)
+
+    def quant(q, sc, t):
+        op("V", lambda: v.quantize_mx(T[q][:], T[sc][:], T[t][:]), [reg(t)], [reg(q), reg(sc)])
+
+    dma("Y", T.X0[:], T.x[:], [], [reg("X0")])
+    dma("S", T.UT[:], T.u[:], [], [reg("UT")])
+    dma("Y", T.FLI[:], T.fl[:], [], [reg("FLI")])
+    dma("S", T.VT[:], T.v[:], [], [reg("VT")])
+    dma("Y", u8(T.WQ[:]), T.wc[:], [], [reg("WQ")])
+    dma("S", T.WS[:], T.ws[:], [], [reg("WS")])
+
+    op("G", lambda: g.iota(T.I1[:], [[1, C]], 128, -1), [], [reg("I1")])
+    op("G", lambda: g.iota(T.OI[:], [[16, 8]], 0, 0), [], [reg("OI")])
+    op("G", lambda: g.iota(T.IOS[:], [[1, C]], -160, 0, allow_small_or_imprecise_dtypes=True), [], [reg("IOS")])
+    for lo, hi, base, st in ((320, 416, 160, 1), (416, 544, 256, 2), (544, 640, 512, 4)):
+        op("G", lambda: g.iota(T.FW1[:, lo:hi], [[st, hi - lo]], base, 0, allow_small_or_imprecise_dtypes=True), [], [reg("FW1", lo, hi)])
+    op("V", lambda: v.memset(T.ET[:], 0.0), [], [reg("ET")])
+    op("V", lambda: v.tensor_scalar(T.IB[:], T.I1[:], 15, None, A.bitwise_and), [reg("I1")], [reg("IB")])
+    op("V", lambda: v.tensor_scalar(T.MSK[:], T.IB[:], 0, None, A.is_equal), [reg("IB")], [reg("MSK")])
+    op("V", lambda: v.tensor_scalar(T.NMS[:], T.IB[:], 0, None, A.not_equal), [reg("IB")], [reg("NMS")])
+    op("V", lambda: v.tensor_copy(T.UO[:], T.OI[:]), [reg("OI")], [reg("UO")])
+    quant("UQ", "US", "UT")
+    op("V", lambda: v.tensor_copy(u32(T.UQ2[:]), u32(T.UQ[:]).indirect(T.UO[:])), [reg("UQ"), reg("UO")], [reg("UQ2")])
+    op("V", lambda: v.tensor_copy(T.US2[:], T.US[:].indirect(T.UO[:])), [reg("US"), reg("UO")], [reg("US2")])
+    quant("QX0", "SX0", "X0")
+    for b in range(4):
+        op("V", lambda: v.tensor_scalar(T.ET[:, 512 * b + b:512 * b + 512:4], T.I1[:, 0:128], 128, 0.5, A.is_equal, A.mult),
+           [reg("I1")], [reg("ET", 512 * b, 512 * b + 512)])
+
+    sc_of_f = {}
+    for r, m in enumerate(MASK):
+        dst = T.cores[rank ^ m]
+        n_ = lambda k: k + str(r)
+        X, QX, SX, FS, FT, FI, F4, PK, LP, LQ, LS = [n_(k) for k in ("X", "QX", "SX", "FS", "FT", "FI", "F4", "PK", "LP", "LQ", "LS")]
+        XF, QF, SF, F, M, Z, QZ, SZ, PW, WN, TB, TF, AT, AI = [n_(k) for k in ("XF", "QF", "SF", "F", "M", "Z", "QZ", "SZ", "PW", "WN", "TB", "TF", "AT", "AI")]
+        nxt = str(r + 1)
+
+        mm(4, "UQ2", "US2", 0, QX, SX)
+        if r == 0:
+            quant("EQ", "ES", "ET")
+            op("V", lambda: v.tensor_scalar(T[PK][:, 0:20], T.FLI[:], -160.0, None, A.add), [reg("FLI")], [reg(PK, 0, 20)])
+        else:
+            ps = str(r - 1)
+            gather_masked(T["FS" + ps][:], reg("FS" + ps), T["AT" + ps][:], reg("AT" + ps))
+            scan()
+            sample(T[PK][:, 0:20], reg(PK, 0, 20), 1.0, 0.0)
+        for b in range(4):
+            mm(b, "EQ", "ES", 128 * b, QX, SX)
+        op("V", lambda: v.tensor_tensor(T.MK[:], T.PS[:, 2048:2048 + C], T.MSK[:], A.mult), [bank(4), reg("MSK")], [reg("MK")])
+        scan()
+        op("V", lambda: v.tensor_scalar(T[PK][:, 20:40], T.SC[:, 15:C:16], 0.0, None, A.is_gt), [reg("SC")], [reg(PK, 20, 40)])
+        send(dst, T[LP][:], T[PK][:], [reg(PK)], reg(LP), n_("apk"))
+        send(dst, u8(T[LQ][:]), u8(T[QX][:]), [reg(QX)], reg(LQ), n_("aq"))
+        send(dst, T[LS][:], T[SX][:], [reg(SX)], reg(LS), n_("asc"))
+
+        op("V", lambda: v.tensor_scalar(T[FT][:], T[PK][:, 0:20], 160.0, None, A.add), [reg(PK, 0, 20)], [reg(FT)])
+        for t in range(4):
+            op("V", lambda: v.tensor_scalar(T[F4][:, 20 * t:20 * t + 20], T[PK][:, 0:20], 4.0, 640.0 + t, A.mult, A.add),
+               [reg(PK, 0, 20)], [reg(F4, 20 * t, 20 * t + 20)])
+        for t in range(4):
+            gather_s(T[XF][:, t:4 * C:4], reg(XF, 0, 4 * C, t), T[X][:], reg(X), T[F4][:, 20 * t:20 * t + 20], reg(F4, 20 * t, 20 * t + 20))
+        for b in range(4):
+            op("V", lambda: v.tensor_copy(T[F][:, C * b:C * b + C], T.PS[:, 512 * b:512 * b + C]), [bank(b)], [reg(F, C * b, C * b + C)])
+        if r == 0:
+            op("V", lambda: v.tensor_tensor(T.MK[:], T.IOS[:], T.MSK[:], A.mult), [reg("IOS"), reg("MSK")], [reg("MK")])
+            scan()
+            sample(T.ATS[:], reg("ATS"), 1.0, 0.0)
+        quant(QF, SF, XF)
+        for b in range(4):
+            mm(4 + b, "EQ", "ES", 128 * b, QF, SF, True, False)
+        for b in range(4):
+            mm(4 + b, "EQ", "ES", 128 * b, LQ, LS, False, True)
+        if r == 0:
+            gather_s(T[FS][:], reg(FS), T.IOS[:], reg("IOS"), T[FT][:], reg(FT))
+            op("V", lambda: v.tensor_copy(T.AI3[:].indirect(T[FT][:]), T.IOS[:]), [reg("IOS"), reg(FT)], [reg("AI3")])
+            op("V", lambda: v.tensor_tensor(T.MK[:], T.AI3[:], T.MSK[:], A.mult), [reg("AI3"), reg("MSK")], [reg("MK")])
+            scan()
+            sample(T[FI][:], reg(FI), 1.0, 160.0)
+
+        def tf(i):
+            return T[TF][:, 20 * i:20 * i + 20]
+
+        def rf(i):
+            return reg(TF, 20 * i, 20 * i + 20)
+
+        def tb(i):
+            return T[TB][:, 20 * i:20 * i + 20]
+
+        def rb(i):
+            return reg(TB, 20 * i, 20 * i + 20)
+        es, be = T[LP][:, 0:20], T[LP][:, 20:40]
+        op("V", lambda: v.tensor_tensor(tf(0), be, T[PK][:, 20:40], A.not_equal), [reg(LP), reg(PK, 20, 40)], [rf(0)])
+        op("V", lambda: v.tensor_tensor(tf(1), T.ATS[:], es, A.subtract), [reg(LP), reg("ATS")], [rf(1)])
+        op("V", lambda: v.tensor_tensor(tf(2), tf(1), tf(0), A.mult), [rf(0), rf(1)], [rf(2)])
+        op("V", lambda: v.tensor_tensor(tf(3), tf(2), es, A.add), [rf(2), reg(LP)], [rf(3)])
+        op("V", lambda: v.tensor_scalar(tb(0), tf(3), 160.0, None, A.add), [rf(3)], [rb(0)])
+
+        def slot(k):
+            return T[WN][:, C * k:C * k + C], reg(WN, C * k, C * k + C)
+        w, wr_ = slot(0)
+        gather_s(w, wr_, T.IOS[:], reg("IOS"), tb(0), rb(0))
+        op("V", lambda: v.tensor_scalar(tf(4), tf(1), -1.0, -320.0, A.mult, A.add), [rf(1)], [rf(4)])
+        op("V", lambda: v.tensor_tensor(tf(5), tf(4), tf(0), A.mult), [rf(4), rf(0)], [rf(5)])
+        op("V", lambda: v.tensor_tensor(tf(6), tf(5), T.ATS[:], A.add), [rf(5), reg("ATS")], [rf(6)])
+        op("V", lambda: v.tensor_scalar(tb(1), tf(6), 480.0, None, A.add), [rf(6)], [rb(1)])
+        if r == 0:
+            op("V", lambda: v.memset(T.FW2[:, C:FW2W], 0.0), [], [reg("FW2", C, FW2W)])
+            for lo, hi, st, a0, a1 in ((320, 416, 1, 0, 96), (416, 672, 2, 96, 224), (672, 1056, 4, 224, 320)):
+                op("V", lambda: v.tensor_copy(T.FW2[:, lo:hi:st], T.IOS[:, a0:a1]), [reg("IOS")], [reg("FW2", lo, hi)])
+
+        def evac_m(b):
+            op("S", lambda: s.activation(T[M][:, C * b:C * b + C], T.PS[:, 2048 + 512 * b:2048 + 512 * b + C], COPY), [bank(4 + b)], [reg(M, C * b, C * b + C)])
+        nslot, cur, mb = 1, 0, 0
+        pt, pw = 1, 1
+        for k, nS in enumerate(SCHED):
+            tcur = cur
+            gather_masked(w, wr_, tb(tcur), rb(tcur))
+            for i in range(nS):
+                if k == len(SCHED) - 1 and i == nS - 1:
+                    w2, wr2 = T.FW1[:, 0:C], reg("FW1", 0, C)
+                else:
+                    w2, wr2 = slot(nslot)
+                    nslot += 1
+                gather_s(w2, wr2, w, wr_, tb(tcur), rb(tcur))
+                w, wr_ = w2, wr2
+            scan()
+            sample(tb(k + 2), rb(k + 2), 1.0, 160.0)
+            cur = k + 2
+            pt, pw = pt + pw, pw + nS * pt
+            if nS == 1:
+                evac_m(mb)
+                mb += 1
+        gather_masked(T.FW1[:], reg("FW1"), tb(1), rb(1))
+        gather_s(T.FW2[:, 0:C], reg("FW2", 0, C), w, wr_, tb(cur), rb(cur))
+        while mb < 4:
+            evac_m(mb)
+            mb += 1
+        scan()
+        fin = len(SCHED) + 2
+        sample(tb(fin), rb(fin), 1.0, 160.0)
+        assert pw + (pw + pt) >= C - 1
+        gather_masked(T.FW2[:], reg("FW2"), tb(fin), rb(fin))
+        scan()
+        sample(T[AT][:], reg(AT), 1.0, 160.0)
+
+        def plane(name, b):
+            return T[name][:, C * b:C * b + C], reg(name, C * b, C * b + C)
+        mw, mr = plane(M, 0)
+        op("V", lambda: v.tensor_copy(T[Z][:, 0:4 * C:4], mw.indirect(T[AT][:])), [mr, reg(AT)], [reg(Z, 0, 4 * C, 0)])
+        for b in range(1, 4):
+            mw, mr = plane(M, b)
+            gather_s(T[Z][:, b:4 * C:4], reg(Z, 0, 4 * C, b), mw, mr, T[AT][:], reg(AT))
+        op("V", lambda: v.tensor_copy(T[AI][:].indirect(T[AT][:]), T.IOS[:]), [reg("IOS"), reg(AT)], [reg(AI)])
+        quant(QZ, SZ, Z)
+        for b in range(4):
+            mm(b, "WQ", "WS", 128 * b, QZ, SZ)
+        gather_s(T["FS" + nxt][:], reg("FS" + nxt), T[FS][:], reg(FS), T[AT][:], reg(AT))
+        gather_masked(T[AI][:], reg(AI), T[FI][:], reg(FI))
+        scan()
+        sample(T["FI" + nxt][:], reg("FI" + nxt), 1.0, 160.0)
+        for b in range(4):
+            pw_, pr = plane(PW, b)
+            op("S", lambda: s.activation(pw_, T.PS[:, 512 * b:512 * b + C], COPY, scale=0.015625), [bank(b)], [pr])
+        for b in range(4):
+            pw_, pr = plane(PW, b)
+            fw_, fr = plane(F, b)
+            op("V", lambda: v.tensor_tensor(T["X" + nxt][:, b:4 * C:4], pw_.indirect(T["FI" + nxt][:]), fw_, A.add),
+               [pr, reg("FI" + nxt), fr], [reg("X" + nxt, 0, 4 * C, b)])
+        quant("QX" + nxt, "SX" + nxt, "X" + nxt)
+        if r == 0:
+            quant("VQ", "VS", "VT")
+
+    mm(4, "VQ", "VS", 0, "QX3", "SX3")
+    dma("Y", T.oc[:], u8(T.QX3[:]), [reg("QX3")], [])
+    for k in range(4):
+        dma("Y" if k % 2 else "S", T.osc[4 * k:4 * k + 4, :], T.SX3[32 * k:32 * k + 4, :], [reg("SX3")], [])
+    op("V", lambda: v.tensor_scalar(T.LNF[:], T.FS3[:], 160.0, None, A.add), [reg("FS3")], [reg("LNF")])
+    op("V", lambda: v.tensor_copy(T.YS[:], T.PS[:, 2048:2048 + C]), [bank(4)], [reg("YS")])
+    dma("S", T.ln[:], T.LNF[0:128:16, :], [reg("LNF")], [])
+    dma("Y", T.y[:], T.YS[:], [reg("YS")], [])
+    for sem, val in count.items():
+        g.wait_ge(T.sem[sem], val)

@@ -2,13 +2,16 @@ from concourse.mybir import dt, AluOpType, ActivationFunctionType
 
 C = 320
 MASK = [1, 2, 4]
-SCHED = [2, 2, 2, 1, 1, 1]
-NW = 1 + sum(SCHED)
+STAGES = [2, 2, 2]
+LAST = 1
+NW = 1 + sum(STAGES) + len(STAGES)
 FW2W = 1056
 
 SCRATCH = {
     "I1": ("sbuf", [128, C], "int32"), "IB": ("sbuf", [128, C], "int32"),
     "IOS": ("sbuf", [128, C], "bfloat16"), "MSK": ("sbuf", [128, C], "bfloat16"), "NMS": ("sbuf", [128, C], "bfloat16"),
+    "PI": ("sbuf", [128, 20], "int32"), "CI": ("sbuf", [128, 20], "int32"), "PA": ("sbuf", [128, 20], "int32"),
+    "DG": ("sbuf", [128, 128], "bfloat16"),
     "OI": ("sbuf", [128, 8], "int32"), "UO": ("sbuf", [128, 8], "uint16"),
     "ATS": ("sbuf", [128, 20], "float32"),
     "ET": ("sbuf", [128, 2048], "bfloat16"),
@@ -22,6 +25,7 @@ SCRATCH = {
     "AI3": ("sbuf", [128, C], "bfloat16"),
     "FW1": ("sbuf", [128, 640], "bfloat16"), "FW2": ("sbuf", [128, FW2W], "bfloat16"),
     "MK": ("sbuf", [128, C], "bfloat16"), "SC": ("sbuf", [128, C], "bfloat16"),
+    "MK2": ("sbuf", [128, C], "bfloat16"), "SC2": ("sbuf", [128, C], "bfloat16"),
     "LNF": ("sbuf", [128, C], "float32"), "YS": ("sbuf", [128, C], "float32"),
     "PS": ("psum", [128, 4096], "float32"),
 }
@@ -30,25 +34,25 @@ for _r in range(4):
         "X%d" % _r: ("sbuf", [128, 4 * C], "bfloat16"),
         "QX%d" % _r: ("sbuf", [128, C], "float8_e4m3fn_x4"), "SX%d" % _r: ("sbuf", [128, C], "uint8"),
         "FS%d" % _r: ("sbuf", [128, C], "bfloat16"),
-        "FT%d" % _r: ("sbuf", [128, 20], "uint16"), "FI%d" % _r: ("sbuf", [128, 20], "uint16"),
-        "F4%d" % _r: ("sbuf", [128, 80], "uint16"),
-        "PK%d" % _r: ("sbuf", [128, 40], "bfloat16"),
+        "FI%d" % _r: ("sbuf", [128, 20], "uint16"),
     })
 for _r in range(3):
     SCRATCH.update({
-        "LP%d" % _r: ("sbuf", [128, 40], "bfloat16"),
+        "F4%d" % _r: ("sbuf", [128, 80], "uint16"),
+        "PK%d" % _r: ("sbuf", [128, 40], "bfloat16"), "LP%d" % _r: ("sbuf", [128, 40], "bfloat16"),
         "LQ%d" % _r: ("sbuf", [128, C], "float8_e4m3fn_x4"), "LS%d" % _r: ("sbuf", [128, C], "uint8"),
         "XF%d" % _r: ("sbuf", [128, 4 * C], "bfloat16"),
         "QF%d" % _r: ("sbuf", [128, C], "float8_e4m3fn_x4"), "SF%d" % _r: ("sbuf", [128, C], "uint8"),
-        "F%d" % _r: ("sbuf", [128, 4 * C], "bfloat16"), "M%d" % _r: ("sbuf", [128, 4 * C], "bfloat16"),
+        "F%d" % _r: ("sbuf", [128, 3 * C], "bfloat16"), "M%d" % _r: ("sbuf", [128, 4 * C], "bfloat16"),
         "Z%d" % _r: ("sbuf", [128, 4 * C], "bfloat16"),
         "QZ%d" % _r: ("sbuf", [128, C], "float8_e4m3fn_x4"), "SZ%d" % _r: ("sbuf", [128, C], "uint8"),
-        "PW%d" % _r: ("sbuf", [128, 4 * C], "float32"),
+        "PW%d" % _r: ("sbuf", [128, 4 * C], "float32"), "B3%d" % _r: ("sbuf", [128, C], "float32"),
         "WN%d" % _r: ("sbuf", [128, C * NW], "bfloat16"),
         "TB%d" % _r: ("sbuf", [128, 20 * 12], "uint16"), "TF%d" % _r: ("sbuf", [128, 20 * 10], "float32"),
         "AT%d" % _r: ("sbuf", [128, 20], "uint16"), "AI%d" % _r: ("sbuf", [128, C], "bfloat16"),
     })
-SEMAPHORES = ["sV", "sS", "sP", "sG", "lsent"] + ["d%d" % i for i in range(16)] + [k + str(r) for r in range(3) for k in ("apk", "aq", "asc")]
+SCRATCH["FT0"] = ("sbuf", [128, 20], "uint16")
+SEMAPHORES = ["sV", "sS", "sP", "sG", "lsent", "apl"] + ["d%d" % i for i in range(16)] + [k + str(r) for r in range(3) for k in ("apk", "aq", "asc")]
 
 
 def rank_program(g, core, T, topo):
@@ -124,14 +128,11 @@ def rank_program(g, core, T, topo):
     def send(dst, out, in_, rd, land, sem):
         deps("G", rd, [], True)
         rid, pid = topo.addr(dst, core)
-        mask = topo.mask(core, dst)
-        n = len(topo.engines(core, dst))
-        g.remote_dma(out, in_, T.sem[sem], T.sem["lsent"], pid, rid, mask)
-        count["lsent"] = count.get("lsent", 0) + n
-        arrives = len(topo.engines(dst, core))
-        count[sem] = arrives
-        behind[(sem, arrives)] = {}
-        writers.setdefault(land[0], []).append((land, (sem, arrives), "far"))
+        g.remote_dma(out, in_, T.sem[sem], T.sem["lsent"], pid, rid, topo.mask(core, dst))
+        count["lsent"] = count.get("lsent", 0) + len(topo.engines(core, dst))
+        count[sem] = len(topo.engines(dst, core))
+        behind[(sem, count[sem])] = {}
+        writers.setdefault(land[0], []).append((land, (sem, count[sem]), "far"))
 
     def u8(ap):
         return ap.bitcast(dt.uint8)
@@ -139,19 +140,17 @@ def rank_program(g, core, T, topo):
     def u32(ap):
         return ap.bitcast(dt.uint32)
 
-    def gather_masked(win, winreg, tab, tabreg):
-        op("V", lambda: v.tensor_tensor(T.MK[:], win.indirect(tab), T.MSK[:], A.mult), [winreg, tabreg, reg("MSK")], [reg("MK")])
+    def gather_masked(win, winreg, tab, tabreg, mk="MK"):
+        op("V", lambda: v.tensor_tensor(T[mk][:], win.indirect(tab), T.MSK[:], A.mult), [winreg, tabreg, reg("MSK")], [reg(mk)])
 
-    def scan():
-        op("V", lambda: v.tensor_tensor_scan(T.SC[:], T.NMS[:], T.MK[:], 0.0, A.mult, A.add), [reg("MK"), reg("NMS")], [reg("SC")])
+    def scan(mk="MK", sc="SC"):
+        op("V", lambda: v.tensor_tensor_scan(T[sc][:], T.NMS[:], T[mk][:], 0.0, A.mult, A.add), [reg(mk), reg("NMS")], [reg(sc)])
 
-    def sample(out, outreg, mul, add):
-        if mul == 1.0 and add == 0.0:
-            op("V", lambda: v.tensor_copy(out, T.SC[:, 15:C:16]), [reg("SC")], [outreg])
-        elif mul == 1.0:
-            op("V", lambda: v.tensor_scalar(out, T.SC[:, 15:C:16], add, None, A.add), [reg("SC")], [outreg])
+    def sample(out, outreg, add, sc="SC"):
+        if add == 0.0:
+            op("V", lambda: v.tensor_copy(out, T[sc][:, 15:C:16]), [reg(sc)], [outreg])
         else:
-            op("V", lambda: v.tensor_scalar(out, T.SC[:, 15:C:16], mul, add, A.mult, A.add), [reg("SC")], [outreg])
+            op("V", lambda: v.tensor_scalar(out, T[sc][:, 15:C:16], add, None, A.add), [reg(sc)], [outreg])
 
     def gather_s(out, outreg, win, winreg, tab, tabreg):
         op("S", lambda: s.activation(out, win.indirect(tab), COPY), [winreg, tabreg], [outreg])
@@ -176,71 +175,96 @@ def rank_program(g, core, T, topo):
 
     op("G", lambda: g.iota(T.I1[:], [[1, C]], 128, -1), [], [reg("I1")])
     op("G", lambda: g.iota(T.OI[:], [[16, 8]], 0, 0), [], [reg("OI")])
+    op("G", lambda: g.iota(T.PI[:], [[0, 20]], 0, 1), [], [reg("PI")])
+    op("G", lambda: g.iota(T.CI[:], [[16, 20]], -160, 0), [], [reg("CI")])
     op("G", lambda: g.iota(T.IOS[:], [[1, C]], -160, 0, allow_small_or_imprecise_dtypes=True), [], [reg("IOS")])
-    for lo, hi, base, st in ((320, 416, 160, 1), (416, 544, 256, 2), (544, 640, 512, 4)):
-        op("G", lambda: g.iota(T.FW1[:, lo:hi], [[st, hi - lo]], base, 0, allow_small_or_imprecise_dtypes=True), [], [reg("FW1", lo, hi)])
     op("V", lambda: v.memset(T.ET[:], 0.0), [], [reg("ET")])
     op("V", lambda: v.tensor_scalar(T.IB[:], T.I1[:], 15, None, A.bitwise_and), [reg("I1")], [reg("IB")])
-    op("V", lambda: v.tensor_scalar(T.MSK[:], T.IB[:], 0, None, A.is_equal), [reg("IB")], [reg("MSK")])
-    op("V", lambda: v.tensor_scalar(T.NMS[:], T.IB[:], 0, None, A.not_equal), [reg("IB")], [reg("NMS")])
     op("V", lambda: v.tensor_copy(T.UO[:], T.OI[:]), [reg("OI")], [reg("UO")])
+    op("V", lambda: v.tensor_scalar(T.MSK[:], T.IB[:], 0, None, A.is_equal), [reg("IB")], [reg("MSK")])
+    op("V", lambda: v.tensor_scalar(T.PK0[:, 0:20], T.FLI[:], -160.0, None, A.add), [reg("FLI")], [reg("PK0", 0, 20)])
+    send(T.cores[rank ^ MASK[0]], T.LP0[:, 0:20], T.PK0[:, 0:20], [reg("PK0", 0, 20)], reg("LP0", 0, 20), "apl")
+    for lo, hi, base, st in ((320, 416, 160, 1), (416, 544, 256, 2), (544, 640, 512, 4)):
+        op("G", lambda: g.iota(T.FW1[:, lo:hi], [[st, hi - lo]], base, 0, allow_small_or_imprecise_dtypes=True), [], [reg("FW1", lo, hi)])
     quant("UQ", "US", "UT")
+    op("S", lambda: s.activation(T.US2[:], T.US[:].indirect(T.UO[:]), COPY), [reg("US"), reg("UO")], [reg("US2")])
     op("V", lambda: v.tensor_copy(u32(T.UQ2[:]), u32(T.UQ[:]).indirect(T.UO[:])), [reg("UQ"), reg("UO")], [reg("UQ2")])
-    op("V", lambda: v.tensor_copy(T.US2[:], T.US[:].indirect(T.UO[:])), [reg("US"), reg("UO")], [reg("US2")])
     quant("QX0", "SX0", "X0")
+    for lo in range(C, FW2W, C):
+        n = min(C, FW2W - lo)
+        op("S", lambda: s.activation(T.FW2[:, lo:lo + n], T.IOS[:, 0:n], COPY), [reg("IOS")], [reg("FW2", lo, lo + n)])
+    for lo, hi, st, a0, a1 in ((416, 672, 2, 96, 224), (672, 1056, 4, 224, 320)):
+        op("S", lambda: s.activation(T.FW2[:, lo:hi:st], T.IOS[:, a0:a1], COPY), [reg("IOS")], [reg("FW2", lo, hi)])
+    op("V", lambda: v.tensor_scalar(T.NMS[:], T.MSK[:], 0.0, None, A.is_equal), [reg("MSK")], [reg("NMS")])
+    op("V", lambda: v.tensor_scalar(T.DG[:], T.I1[:, 0:128], 128, 0.5, A.is_equal, A.mult), [reg("I1")], [reg("DG")])
     for b in range(4):
-        op("V", lambda: v.tensor_scalar(T.ET[:, 512 * b + b:512 * b + 512:4], T.I1[:, 0:128], 128, 0.5, A.is_equal, A.mult),
-           [reg("I1")], [reg("ET", 512 * b, 512 * b + 512)])
+        op("S", lambda: s.activation(T.ET[:, 512 * b + b:512 * b + 512:4], T.DG[:], COPY), [reg("DG")], [reg("ET", 512 * b, 512 * b + 512)])
 
-    sc_of_f = {}
-    for r, m in enumerate(MASK):
-        dst = T.cores[rank ^ m]
-        n_ = lambda k: k + str(r)
-        X, QX, SX, FS, FT, FI, F4, PK, LP, LQ, LS = [n_(k) for k in ("X", "QX", "SX", "FS", "FT", "FI", "F4", "PK", "LP", "LQ", "LS")]
-        XF, QF, SF, F, M, Z, QZ, SZ, PW, WN, TB, TF, AT, AI = [n_(k) for k in ("XF", "QF", "SF", "F", "M", "Z", "QZ", "SZ", "PW", "WN", "TB", "TF", "AT", "AI")]
-        nxt = str(r + 1)
-
-        mm(4, "UQ2", "US2", 0, QX, SX)
-        if r == 0:
-            quant("EQ", "ES", "ET")
-            op("V", lambda: v.tensor_scalar(T[PK][:, 0:20], T.FLI[:], -160.0, None, A.add), [reg("FLI")], [reg(PK, 0, 20)])
-        else:
-            ps = str(r - 1)
-            gather_masked(T["FS" + ps][:], reg("FS" + ps), T["AT" + ps][:], reg("AT" + ps))
-            scan()
-            sample(T[PK][:, 0:20], reg(PK, 0, 20), 1.0, 0.0)
-        for b in range(4):
-            mm(b, "EQ", "ES", 128 * b, QX, SX)
-        op("V", lambda: v.tensor_tensor(T.MK[:], T.PS[:, 2048:2048 + C], T.MSK[:], A.mult), [bank(4), reg("MSK")], [reg("MK")])
-        scan()
-        op("V", lambda: v.tensor_scalar(T[PK][:, 20:40], T.SC[:, 15:C:16], 0.0, None, A.is_gt), [reg("SC")], [reg(PK, 20, 40)])
-        send(dst, T[LP][:], T[PK][:], [reg(PK)], reg(LP), n_("apk"))
-        send(dst, u8(T[LQ][:]), u8(T[QX][:]), [reg(QX)], reg(LQ), n_("aq"))
-        send(dst, T[LS][:], T[SX][:], [reg(SX)], reg(LS), n_("asc"))
-
-        op("V", lambda: v.tensor_scalar(T[FT][:], T[PK][:, 0:20], 160.0, None, A.add), [reg(PK, 0, 20)], [reg(FT)])
+    def laid(r):
+        F4, PK, XF, X = ["%s%d" % (k, r) for k in ("F4", "PK", "XF", "X")]
         for t in range(4):
             op("V", lambda: v.tensor_scalar(T[F4][:, 20 * t:20 * t + 20], T[PK][:, 0:20], 4.0, 640.0 + t, A.mult, A.add),
                [reg(PK, 0, 20)], [reg(F4, 20 * t, 20 * t + 20)])
         for t in range(4):
             gather_s(T[XF][:, t:4 * C:4], reg(XF, 0, 4 * C, t), T[X][:], reg(X), T[F4][:, 20 * t:20 * t + 20], reg(F4, 20 * t, 20 * t + 20))
-        for b in range(4):
-            op("V", lambda: v.tensor_copy(T[F][:, C * b:C * b + C], T.PS[:, 512 * b:512 * b + C]), [bank(b)], [reg(F, C * b, C * b + C)])
+
+    for r, m in enumerate(MASK):
+        dst = T.cores[rank ^ m]
+        n_ = lambda k: k + str(r)
+        X, QX, SX, FS, FI, F4, PK, LP, LQ, LS = [n_(k) for k in ("X", "QX", "SX", "FS", "FI", "F4", "PK", "LP", "LQ", "LS")]
+        XF, QF, SF, F, M, Z, QZ, SZ, PW, WN, TB, TF, AT, AI, B3 = [n_(k) for k in ("XF", "QF", "SF", "F", "M", "Z", "QZ", "SZ", "PW", "WN", "TB", "TF", "AT", "AI", "B3")]
+        nxt = str(r + 1)
+
+        mm(4, "UQ2", "US2", 0, QX, SX)
         if r == 0:
-            op("V", lambda: v.tensor_tensor(T.MK[:], T.IOS[:], T.MSK[:], A.mult), [reg("IOS"), reg("MSK")], [reg("MK")])
-            scan()
-            sample(T.ATS[:], reg("ATS"), 1.0, 0.0)
+            laid(0)
+        else:
+            ps = str(r - 1)
+            gather_masked(T["FS" + ps][:], reg("FS" + ps), T["AT" + ps][:], reg("AT" + ps), "MK2")
+            for b in range(4):
+                mm(b, "EQ", "ES", 128 * b, QX, SX)
+        op("V", lambda: v.tensor_tensor(T.MK[:], T.PS[:, 2048:2048 + C], T.MSK[:], A.mult), [bank(4), reg("MSK")], [reg("MK")])
+        if r > 0:
+            scan("MK2", "SC2")
+        else:
+            op("V", lambda: v.tensor_scalar(T.PA[:], T.PI[:], 15, None, A.bitwise_and), [reg("PI")], [reg("PA")])
+        scan()
+        if r > 0:
+            sample(T[PK][:, 0:20], reg(PK, 0, 20), 0.0, "SC2")
+        else:
+            op("V", lambda: v.tensor_tensor(T.ATS[:], T.PA[:], T.CI[:], A.add), [reg("PA"), reg("CI")], [reg("ATS")])
+        op("V", lambda: v.tensor_scalar(T[PK][:, 20:40], T.SC[:, 15:C:16], 0.0, None, A.is_gt), [reg("SC")], [reg(PK, 20, 40)])
+        if r == 0:
+            send(dst, T[LP][:, 20:40], T[PK][:, 20:40], [reg(PK, 20, 40)], reg(LP, 20, 40), n_("apk"))
+        else:
+            send(dst, T[LP][:], T[PK][:], [reg(PK)], reg(LP), n_("apk"))
+        send(dst, u8(T[LQ][:]), u8(T[QX][:]), [reg(QX)], reg(LQ), n_("aq"))
+        send(dst, T[LS][:], T[SX][:], [reg(SX)], reg(LS), n_("asc"))
+
+        if r > 0:
+            laid(r)
+        else:
+            quant("EQ", "ES", "ET")
+            for b in range(4):
+                mm(b, "EQ", "ES", 128 * b, QX, SX)
+            op("V", lambda: v.tensor_scalar(T.FT0[:], T[PK][:, 0:20], 160.0, None, A.add), [reg(PK, 0, 20)], [reg("FT0")])
+        for b in range(3):
+            if r == 0:
+                op("S", lambda: s.activation(T[F][:, C * b:C * b + C], T.PS[:, 512 * b:512 * b + C], COPY), [bank(b)], [reg(F, C * b, C * b + C)])
+            else:
+                op("V", lambda: v.tensor_copy(T[F][:, C * b:C * b + C], T.PS[:, 512 * b:512 * b + C]), [bank(b)], [reg(F, C * b, C * b + C)])
+        if r == 0:
+            op("V", lambda: v.tensor_copy(T.AI3[:].indirect(T.FT0[:]), T.IOS[:]), [reg("IOS"), reg("FT0")], [reg("AI3")])
         quant(QF, SF, XF)
         for b in range(4):
             mm(4 + b, "EQ", "ES", 128 * b, QF, SF, True, False)
         for b in range(4):
             mm(4 + b, "EQ", "ES", 128 * b, LQ, LS, False, True)
         if r == 0:
-            gather_s(T[FS][:], reg(FS), T.IOS[:], reg("IOS"), T[FT][:], reg(FT))
-            op("V", lambda: v.tensor_copy(T.AI3[:].indirect(T[FT][:]), T.IOS[:]), [reg("IOS"), reg(FT)], [reg("AI3")])
+            gather_s(T[FS][:], reg(FS), T.IOS[:], reg("IOS"), T.FT0[:], reg("FT0"))
             op("V", lambda: v.tensor_tensor(T.MK[:], T.AI3[:], T.MSK[:], A.mult), [reg("AI3"), reg("MSK")], [reg("MK")])
             scan()
-            sample(T[FI][:], reg(FI), 1.0, 160.0)
+            sample(T[FI][:], reg(FI), 160.0)
 
         def tf(i):
             return T[TF][:, 20 * i:20 * i + 20]
@@ -253,60 +277,61 @@ def rank_program(g, core, T, topo):
 
         def rb(i):
             return reg(TB, 20 * i, 20 * i + 20)
-        es, be = T[LP][:, 0:20], T[LP][:, 20:40]
-        op("V", lambda: v.tensor_tensor(tf(0), be, T[PK][:, 20:40], A.not_equal), [reg(LP), reg(PK, 20, 40)], [rf(0)])
-        op("V", lambda: v.tensor_tensor(tf(1), T.ATS[:], es, A.subtract), [reg(LP), reg("ATS")], [rf(1)])
+        es, be, le, lb = T[LP][:, 0:20], T[LP][:, 20:40], reg(LP, 0, 20), reg(LP, 20, 40)
+        op("V", lambda: v.tensor_tensor(tf(1), T.ATS[:], es, A.subtract), [le, reg("ATS")], [rf(1)])
+        op("V", lambda: v.tensor_tensor(tf(0), be, T[PK][:, 20:40], A.not_equal), [lb, reg(PK, 20, 40)], [rf(0)])
         op("V", lambda: v.tensor_tensor(tf(2), tf(1), tf(0), A.mult), [rf(0), rf(1)], [rf(2)])
-        op("V", lambda: v.tensor_tensor(tf(3), tf(2), es, A.add), [rf(2), reg(LP)], [rf(3)])
+        op("V", lambda: v.tensor_scalar(tf(4), tf(0), -320.0, 480.0, A.mult, A.add), [rf(0)], [rf(4)])
+        op("V", lambda: v.tensor_tensor(tf(3), tf(2), es, A.add), [rf(2), le], [rf(3)])
+        op("V", lambda: v.tensor_tensor(tf(5), T.ATS[:], tf(2), A.subtract), [rf(2), reg("ATS")], [rf(5)])
         op("V", lambda: v.tensor_scalar(tb(0), tf(3), 160.0, None, A.add), [rf(3)], [rb(0)])
 
         def slot(k):
             return T[WN][:, C * k:C * k + C], reg(WN, C * k, C * k + C)
-        w, wr_ = slot(0)
-        gather_s(w, wr_, T.IOS[:], reg("IOS"), tb(0), rb(0))
-        op("V", lambda: v.tensor_scalar(tf(4), tf(1), -1.0, -320.0, A.mult, A.add), [rf(1)], [rf(4)])
-        op("V", lambda: v.tensor_tensor(tf(5), tf(4), tf(0), A.mult), [rf(4), rf(0)], [rf(5)])
-        op("V", lambda: v.tensor_tensor(tf(6), tf(5), T.ATS[:], A.add), [rf(5), reg("ATS")], [rf(6)])
-        op("V", lambda: v.tensor_scalar(tb(1), tf(6), 480.0, None, A.add), [rf(6)], [rb(1)])
-        if r == 0:
-            op("V", lambda: v.memset(T.FW2[:, C:FW2W], 0.0), [], [reg("FW2", C, FW2W)])
-            for lo, hi, st, a0, a1 in ((320, 416, 1, 0, 96), (416, 672, 2, 96, 224), (672, 1056, 4, 224, 320)):
-                op("V", lambda: v.tensor_copy(T.FW2[:, lo:hi:st], T.IOS[:, a0:a1]), [reg("IOS")], [reg("FW2", lo, hi)])
+        H = C // 2
+
+        def both(ob, lo, win, winreg, i):
+            t = T[TB]
+            op("V", lambda: v.tensor_copy(T[ob][:, lo:lo + H], win.indirect(t[:, 20 * i:20 * i + 10])), [winreg, rb(i)], [reg(ob, lo, lo + H)])
+            op("S", lambda: s.activation(T[ob][:, lo + H:lo + C], win.indirect(t[:, 20 * i + 10:20 * i + 20]), COPY), [winreg, rb(i)], [reg(ob, lo + H, lo + C)])
+            return T[ob][:, lo:lo + C], reg(ob, lo, lo + C)
+        w = both(WN, 0, T.IOS[:], reg("IOS"), 0)
+        op("V", lambda: v.tensor_tensor(tf(6), tf(5), tf(4), A.add), [rf(5), rf(4)], [rf(6)])
 
         def evac_m(b):
             op("S", lambda: s.activation(T[M][:, C * b:C * b + C], T.PS[:, 2048 + 512 * b:2048 + 512 * b + C], COPY), [bank(4 + b)], [reg(M, C * b, C * b + C)])
-        nslot, cur, mb = 1, 0, 0
-        pt, pw = 1, 1
-        for k, nS in enumerate(SCHED):
-            tcur = cur
-            gather_masked(w, wr_, tb(tcur), rb(tcur))
-            for i in range(nS):
-                if k == len(SCHED) - 1 and i == nS - 1:
-                    w2, wr2 = T.FW1[:, 0:C], reg("FW1", 0, C)
-                else:
-                    w2, wr2 = slot(nslot)
-                    nslot += 1
-                gather_s(w2, wr2, w, wr_, tb(tcur), rb(tcur))
-                w, wr_ = w2, wr2
+        nslot, cur, pt, pw = 1, 0, 1, 1
+        for k, ahead in enumerate(STAGES):
+            for i in range(ahead):
+                w = both(WN, C * nslot, w[0], w[1], cur)
+                nslot, pw = nslot + 1, pw + pt
+            gather_masked(w[0], w[1], tb(cur), rb(cur))
+            w2 = slot(nslot)
+            gather_s(w2[0], w2[1], w[0], w[1], tb(cur), rb(cur))
+            nslot += 1
+            if k == 0:
+                op("V", lambda: v.tensor_copy(tb(1), tf(6)), [rf(6)], [rb(1)])
             scan()
-            sample(tb(k + 2), rb(k + 2), 1.0, 160.0)
-            cur = k + 2
-            pt, pw = pt + pw, pw + nS * pt
-            if nS == 1:
-                evac_m(mb)
-                mb += 1
+            cur, w = k + 2, w2
+            pt, pw = pt + pw, pw + pt
+            sample(tb(cur), rb(cur), 160.0)
+            if k == len(STAGES) - 1:
+                evac_m(0)
+        for i in range(LAST):
+            ob, lo = ("FW1", 0) if i == LAST - 1 else (WN, C * nslot)
+            w = both(ob, lo, w[0], w[1], cur)
+            pw += pt
+        fin = len(STAGES) + 2
         gather_masked(T.FW1[:], reg("FW1"), tb(1), rb(1))
-        gather_s(T.FW2[:, 0:C], reg("FW2", 0, C), w, wr_, tb(cur), rb(cur))
-        while mb < 4:
-            evac_m(mb)
-            mb += 1
+        gather_s(T.FW2[:, 0:C], reg("FW2", 0, C), w[0], w[1], tb(cur), rb(cur))
         scan()
-        fin = len(SCHED) + 2
-        sample(tb(fin), rb(fin), 1.0, 160.0)
+        sample(tb(fin), rb(fin), 160.0)
         assert pw + (pw + pt) >= C - 1
+        for b in range(1, 4):
+            evac_m(b)
         gather_masked(T.FW2[:], reg("FW2"), tb(fin), rb(fin))
         scan()
-        sample(T[AT][:], reg(AT), 1.0, 160.0)
+        sample(T[AT][:], reg(AT), 160.0)
 
         def plane(name, b):
             return T[name][:, C * b:C * b + C], reg(name, C * b, C * b + C)
@@ -318,21 +343,26 @@ def rank_program(g, core, T, topo):
         op("V", lambda: v.tensor_copy(T[AI][:].indirect(T[AT][:]), T.IOS[:]), [reg("IOS"), reg(AT)], [reg(AI)])
         quant(QZ, SZ, Z)
         for b in range(4):
-            mm(b, "WQ", "WS", 128 * b, QZ, SZ)
+            mm(4 + b, "WQ", "WS", 128 * b, QZ, SZ)
         gather_s(T["FS" + nxt][:], reg("FS" + nxt), T[FS][:], reg(FS), T[AT][:], reg(AT))
         gather_masked(T[AI][:], reg(AI), T[FI][:], reg(FI))
         scan()
-        sample(T["FI" + nxt][:], reg("FI" + nxt), 1.0, 160.0)
+        sample(T["FI" + nxt][:], reg("FI" + nxt), 160.0)
         for b in range(4):
-            pw_, pr = plane(PW, b)
-            op("S", lambda: s.activation(pw_, T.PS[:, 512 * b:512 * b + C], COPY, scale=0.015625), [bank(b)], [pr])
-        for b in range(4):
+            op("S", lambda: s.activation(T[PW][:, C * b:C * b + C], T.PS[:, 2048 + 512 * b:2048 + 512 * b + C], COPY, scale=0.015625),
+               [bank(4 + b)], [reg(PW, C * b, C * b + C)])
+        fi, fir = T["FI" + nxt][:], reg("FI" + nxt)
+        pw3, pr3 = plane(PW, 3)
+        gather_s(T[B3][:], reg(B3), pw3, pr3, fi, fir)
+        for b in range(3):
             pw_, pr = plane(PW, b)
             fw_, fr = plane(F, b)
-            op("V", lambda: v.tensor_tensor(T["X" + nxt][:, b:4 * C:4], pw_.indirect(T["FI" + nxt][:]), fw_, A.add),
-               [pr, reg("FI" + nxt), fr], [reg("X" + nxt, 0, 4 * C, b)])
+            op("V", lambda: v.tensor_tensor(T["X" + nxt][:, b:4 * C:4], pw_.indirect(fi), fw_, A.add),
+               [pr, fir, fr], [reg("X" + nxt, 0, 4 * C, b)])
+        op("V", lambda: v.tensor_tensor(T["X" + nxt][:, 3:4 * C:4], T[B3][:], T.PS[:, 1536:1536 + C], A.add),
+           [reg(B3), bank(3)], [reg("X" + nxt, 0, 4 * C, 3)])
         quant("QX" + nxt, "SX" + nxt, "X" + nxt)
-        if r == 0:
+        if r == 2:
             quant("VQ", "VS", "VT")
 
     mm(4, "VQ", "VS", 0, "QX3", "SX3")

from concourse.mybir import dt, AluOpType, ActivationFunctionType

C = 320
MASK = [1, 2, 4]
STAGES = [2, 2, 2]
LAST = 1
NW = 1 + sum(STAGES) + len(STAGES)
FW2W = 1056

SCRATCH = {
    "I1": ("sbuf", [128, C], "int32"), "IB": ("sbuf", [128, C], "int32"),
    "IOS": ("sbuf", [128, C], "bfloat16"), "MSK": ("sbuf", [128, C], "bfloat16"), "NMS": ("sbuf", [128, C], "bfloat16"),
    "PI": ("sbuf", [128, 20], "int32"), "CI": ("sbuf", [128, 20], "int32"), "PA": ("sbuf", [128, 20], "int32"),
    "DG": ("sbuf", [128, 128], "bfloat16"),
    "OI": ("sbuf", [128, 8], "int32"), "UO": ("sbuf", [128, 8], "uint16"),
    "ATS": ("sbuf", [128, 20], "float32"),
    "ET": ("sbuf", [128, 2048], "bfloat16"),
    "EQ": ("sbuf", [128, 512], "float8_e4m3fn_x4"), "ES": ("sbuf", [128, 512], "uint8"),
    "UT": ("sbuf", [128, 512], "bfloat16"), "VT": ("sbuf", [128, 512], "bfloat16"),
    "UQ": ("sbuf", [128, 128], "float8_e4m3fn_x4"), "US": ("sbuf", [128, 128], "uint8"),
    "UQ2": ("sbuf", [128, 128], "float8_e4m3fn_x4"), "US2": ("sbuf", [128, 128], "uint8"),
    "VQ": ("sbuf", [128, 128], "float8_e4m3fn_x4"), "VS": ("sbuf", [128, 128], "uint8"),
    "WQ": ("sbuf", [128, 512], "float8_e4m3fn_x4"), "WS": ("sbuf", [128, 512], "uint8"),
    "FLI": ("sbuf", [128, 20], "int32"),
    "AI3": ("sbuf", [128, C], "bfloat16"),
    "FW1": ("sbuf", [128, 640], "bfloat16"), "FW2": ("sbuf", [128, FW2W], "bfloat16"),
    "MK": ("sbuf", [128, C], "bfloat16"), "SC": ("sbuf", [128, C], "bfloat16"),
    "MK2": ("sbuf", [128, C], "bfloat16"), "SC2": ("sbuf", [128, C], "bfloat16"),
    "LNF": ("sbuf", [128, C], "float32"), "YS": ("sbuf", [128, C], "float32"),
    "PS": ("psum", [128, 4096], "float32"),
}
for _r in range(4):
    SCRATCH.update({
        "X%d" % _r: ("sbuf", [128, 4 * C], "bfloat16"),
        "QX%d" % _r: ("sbuf", [128, C], "float8_e4m3fn_x4"), "SX%d" % _r: ("sbuf", [128, C], "uint8"),
        "FS%d" % _r: ("sbuf", [128, C], "bfloat16"),
        "FI%d" % _r: ("sbuf", [128, 20], "uint16"),
    })
for _r in range(3):
    SCRATCH.update({
        "F4%d" % _r: ("sbuf", [128, 80], "uint16"),
        "PK%d" % _r: ("sbuf", [128, 40], "bfloat16"), "LP%d" % _r: ("sbuf", [128, 40], "bfloat16"),
        "LQ%d" % _r: ("sbuf", [128, C], "float8_e4m3fn_x4"), "LS%d" % _r: ("sbuf", [128, C], "uint8"),
        "XF%d" % _r: ("sbuf", [128, 4 * C], "bfloat16"),
        "QF%d" % _r: ("sbuf", [128, C], "float8_e4m3fn_x4"), "SF%d" % _r: ("sbuf", [128, C], "uint8"),
        "F%d" % _r: ("sbuf", [128, 3 * C], "bfloat16"), "M%d" % _r: ("sbuf", [128, 4 * C], "bfloat16"),
        "Z%d" % _r: ("sbuf", [128, 4 * C], "bfloat16"),
        "QZ%d" % _r: ("sbuf", [128, C], "float8_e4m3fn_x4"), "SZ%d" % _r: ("sbuf", [128, C], "uint8"),
        "PW%d" % _r: ("sbuf", [128, 4 * C], "float32"), "B3%d" % _r: ("sbuf", [128, C], "float32"),
        "WN%d" % _r: ("sbuf", [128, C * NW], "bfloat16"),
        "TB%d" % _r: ("sbuf", [128, 20 * 12], "uint16"), "TF%d" % _r: ("sbuf", [128, 20 * 10], "float32"),
        "AT%d" % _r: ("sbuf", [128, 20], "uint16"), "AI%d" % _r: ("sbuf", [128, C], "bfloat16"),
    })
SCRATCH["FT0"] = ("sbuf", [128, 20], "uint16")
SEMAPHORES = ["sV", "sS", "sP", "sG", "lsent", "apl"] + ["d%d" % i for i in range(16)] + [k + str(r) for r in range(3) for k in ("apk", "aq", "asc")]


def rank_program(g, core, T, topo):
    rank = T.rank_of(core)
    if rank is None:
        return
    A = AluOpType
    COPY = ActivationFunctionType.Copy
    v, s, pe = g.vector, g.scalar, g.tensor
    queue = {"V": v, "S": s, "P": pe, "G": g, "Y": g.sync}

    count = {}
    known = {q: {} for q in queue}
    behind = {}
    writers, readers = {}, {}

    def reg(name, lo=0, hi=None, lane=None):
        return (name, lo, T[name].shape[1] if hi is None else hi, lane)

    def meet(a, b):
        return a[1] < b[2] and b[1] < a[2] and (a[3] is None or b[3] is None or a[3] == b[3])

    def need(q, toks):
        best = {}
        for (sem, val) in toks:
            if known[q].get(sem, 0) < val and best.get(sem, 0) < val:
                best[sem] = val
        for sem in list(best):
            for sem2, val2 in best.items():
                if sem2 != sem and behind.get((sem2, val2), {}).get(sem, 0) >= best[sem]:
                    best[sem] = 0
                    break
        for sem, val in best.items():
            if val:
                queue[q].wait_ge(T.sem[sem], val)
                known[q][sem] = max(val, known[q].get(sem, 0))
                for k2, v2 in behind.get((sem, val), {}).items():
                    known[q][k2] = max(v2, known[q].get(k2, 0))

    def deps(q, rd, wr, dma):
        toks = []
        for r_ in rd:
            toks += [t for (x, t, e) in writers.get(r_[0], []) if meet(x, r_)]
        for w_ in wr:
            toks += [t for (x, t, e) in writers.get(w_[0], []) if meet(x, w_) and not (q == "P" and e == q)]
            toks += [t for (x, t, e) in readers.get(w_[0], []) if meet(x, w_) and (dma or e != q)]
        need(q, toks)

    def note(q, rd, wr, tok, e):
        behind[tok] = dict(known[q])
        for r_ in rd:
            readers.setdefault(r_[0], []).append((r_, tok, e))
        for w_ in wr:
            writers.setdefault(w_[0], []).append((w_, tok, e))

    def op(q, call, rd, wr):
        deps(q, rd, wr, False)
        sem = "s" + q
        count[sem] = count.get(sem, 0) + 1
        call().then_inc(T.sem[sem], 1)
        note(q, rd, wr, (sem, count[sem]), q)

    ndma = [0]

    def dma(q, out, in_, rd, wr):
        deps(q, rd, wr, True)
        sem = "d%d" % ndma[0]
        ndma[0] += 1
        count[sem] = 16
        queue[q].dma_start(out, in_).then_inc(T.sem[sem], 16)
        note(q, rd, wr, (sem, 16), "dma" + sem)

    def send(dst, out, in_, rd, land, sem):
        deps("G", rd, [], True)
        rid, pid = topo.addr(dst, core)
        g.remote_dma(out, in_, T.sem[sem], T.sem["lsent"], pid, rid, topo.mask(core, dst))
        count["lsent"] = count.get("lsent", 0) + len(topo.engines(core, dst))
        count[sem] = len(topo.engines(dst, core))
        behind[(sem, count[sem])] = {}
        writers.setdefault(land[0], []).append((land, (sem, count[sem]), "far"))

    def u8(ap):
        return ap.bitcast(dt.uint8)

    def u32(ap):
        return ap.bitcast(dt.uint32)

    def gather_masked(win, winreg, tab, tabreg, mk="MK"):
        op("V", lambda: v.tensor_tensor(T[mk][:], win.indirect(tab), T.MSK[:], A.mult), [winreg, tabreg, reg("MSK")], [reg(mk)])

    def scan(mk="MK", sc="SC"):
        op("V", lambda: v.tensor_tensor_scan(T[sc][:], T.NMS[:], T[mk][:], 0.0, A.mult, A.add), [reg(mk), reg("NMS")], [reg(sc)])

    def sample(out, outreg, add, sc="SC"):
        if add == 0.0:
            op("V", lambda: v.tensor_copy(out, T[sc][:, 15:C:16]), [reg(sc)], [outreg])
        else:
            op("V", lambda: v.tensor_scalar(out, T[sc][:, 15:C:16], add, None, A.add), [reg(sc)], [outreg])

    def gather_s(out, outreg, win, winreg, tab, tabreg):
        op("S", lambda: s.activation(out, win.indirect(tab), COPY), [winreg, tabreg], [outreg])

    def mm(bank, lq, ls, lo, rq, rs, start=True, stop=True):
        b0 = 512 * bank
        op("P", lambda: pe.matmul_mx(T.PS[:, b0:b0 + C], T[lq][:, lo:lo + 128], T[ls][:, lo:lo + 128], T[rq][:], T[rs][:], start, stop),
           [reg(lq, lo, lo + 128), reg(ls, lo, lo + 128), reg(rq), reg(rs)], [reg("PS", b0, b0 + 512)])

    def bank(b):
        return reg("PS", 512 * b, 512 * b + 512)

    def quant(q, sc, t):
        op("V", lambda: v.quantize_mx(T[q][:], T[sc][:], T[t][:]), [reg(t)], [reg(q), reg(sc)])

    dma("Y", T.X0[:], T.x[:], [], [reg("X0")])
    dma("S", T.UT[:], T.u[:], [], [reg("UT")])
    dma("Y", T.FLI[:], T.fl[:], [], [reg("FLI")])
    dma("S", T.VT[:], T.v[:], [], [reg("VT")])
    dma("Y", u8(T.WQ[:]), T.wc[:], [], [reg("WQ")])
    dma("S", T.WS[:], T.ws[:], [], [reg("WS")])

    op("G", lambda: g.iota(T.I1[:], [[1, C]], 128, -1), [], [reg("I1")])
    op("G", lambda: g.iota(T.OI[:], [[16, 8]], 0, 0), [], [reg("OI")])
    op("G", lambda: g.iota(T.PI[:], [[0, 20]], 0, 1), [], [reg("PI")])
    op("G", lambda: g.iota(T.CI[:], [[16, 20]], -160, 0), [], [reg("CI")])
    op("G", lambda: g.iota(T.IOS[:], [[1, C]], -160, 0, allow_small_or_imprecise_dtypes=True), [], [reg("IOS")])
    op("V", lambda: v.memset(T.ET[:], 0.0), [], [reg("ET")])
    op("V", lambda: v.tensor_scalar(T.IB[:], T.I1[:], 15, None, A.bitwise_and), [reg("I1")], [reg("IB")])
    op("V", lambda: v.tensor_copy(T.UO[:], T.OI[:]), [reg("OI")], [reg("UO")])
    op("V", lambda: v.tensor_scalar(T.MSK[:], T.IB[:], 0, None, A.is_equal), [reg("IB")], [reg("MSK")])
    op("V", lambda: v.tensor_scalar(T.PK0[:, 0:20], T.FLI[:], -160.0, None, A.add), [reg("FLI")], [reg("PK0", 0, 20)])
    send(T.cores[rank ^ MASK[0]], T.LP0[:, 0:20], T.PK0[:, 0:20], [reg("PK0", 0, 20)], reg("LP0", 0, 20), "apl")
    for lo, hi, base, st in ((320, 416, 160, 1), (416, 544, 256, 2), (544, 640, 512, 4)):
        op("G", lambda: g.iota(T.FW1[:, lo:hi], [[st, hi - lo]], base, 0, allow_small_or_imprecise_dtypes=True), [], [reg("FW1", lo, hi)])
    quant("UQ", "US", "UT")
    op("S", lambda: s.activation(T.US2[:], T.US[:].indirect(T.UO[:]), COPY), [reg("US"), reg("UO")], [reg("US2")])
    op("V", lambda: v.tensor_copy(u32(T.UQ2[:]), u32(T.UQ[:]).indirect(T.UO[:])), [reg("UQ"), reg("UO")], [reg("UQ2")])
    quant("QX0", "SX0", "X0")
    for lo in range(C, FW2W, C):
        n = min(C, FW2W - lo)
        op("S", lambda: s.activation(T.FW2[:, lo:lo + n], T.IOS[:, 0:n], COPY), [reg("IOS")], [reg("FW2", lo, lo + n)])
    for lo, hi, st, a0, a1 in ((416, 672, 2, 96, 224), (672, 1056, 4, 224, 320)):
        op("S", lambda: s.activation(T.FW2[:, lo:hi:st], T.IOS[:, a0:a1], COPY), [reg("IOS")], [reg("FW2", lo, hi)])
    op("V", lambda: v.tensor_scalar(T.NMS[:], T.MSK[:], 0.0, None, A.is_equal), [reg("MSK")], [reg("NMS")])
    op("V", lambda: v.tensor_scalar(T.DG[:], T.I1[:, 0:128], 128, 0.5, A.is_equal, A.mult), [reg("I1")], [reg("DG")])
    for b in range(4):
        op("S", lambda: s.activation(T.ET[:, 512 * b + b:512 * b + 512:4], T.DG[:], COPY), [reg("DG")], [reg("ET", 512 * b, 512 * b + 512)])

    def laid(r):
        F4, PK, XF, X = ["%s%d" % (k, r) for k in ("F4", "PK", "XF", "X")]
        for t in range(4):
            op("V", lambda: v.tensor_scalar(T[F4][:, 20 * t:20 * t + 20], T[PK][:, 0:20], 4.0, 640.0 + t, A.mult, A.add),
               [reg(PK, 0, 20)], [reg(F4, 20 * t, 20 * t + 20)])
        for t in range(4):
            gather_s(T[XF][:, t:4 * C:4], reg(XF, 0, 4 * C, t), T[X][:], reg(X), T[F4][:, 20 * t:20 * t + 20], reg(F4, 20 * t, 20 * t + 20))

    for r, m in enumerate(MASK):
        dst = T.cores[rank ^ m]
        n_ = lambda k: k + str(r)
        X, QX, SX, FS, FI, F4, PK, LP, LQ, LS = [n_(k) for k in ("X", "QX", "SX", "FS", "FI", "F4", "PK", "LP", "LQ", "LS")]
        XF, QF, SF, F, M, Z, QZ, SZ, PW, WN, TB, TF, AT, AI, B3 = [n_(k) for k in ("XF", "QF", "SF", "F", "M", "Z", "QZ", "SZ", "PW", "WN", "TB", "TF", "AT", "AI", "B3")]
        nxt = str(r + 1)

        mm(4, "UQ2", "US2", 0, QX, SX)
        if r == 0:
            laid(0)
        else:
            ps = str(r - 1)
            gather_masked(T["FS" + ps][:], reg("FS" + ps), T["AT" + ps][:], reg("AT" + ps), "MK2")
            for b in range(4):
                mm(b, "EQ", "ES", 128 * b, QX, SX)
        op("V", lambda: v.tensor_tensor(T.MK[:], T.PS[:, 2048:2048 + C], T.MSK[:], A.mult), [bank(4), reg("MSK")], [reg("MK")])
        if r > 0:
            scan("MK2", "SC2")
        else:
            op("V", lambda: v.tensor_scalar(T.PA[:], T.PI[:], 15, None, A.bitwise_and), [reg("PI")], [reg("PA")])
        scan()
        if r > 0:
            sample(T[PK][:, 0:20], reg(PK, 0, 20), 0.0, "SC2")
        else:
            op("V", lambda: v.tensor_tensor(T.ATS[:], T.PA[:], T.CI[:], A.add), [reg("PA"), reg("CI")], [reg("ATS")])
        op("V", lambda: v.tensor_scalar(T[PK][:, 20:40], T.SC[:, 15:C:16], 0.0, None, A.is_gt), [reg("SC")], [reg(PK, 20, 40)])
        if r == 0:
            send(dst, T[LP][:, 20:40], T[PK][:, 20:40], [reg(PK, 20, 40)], reg(LP, 20, 40), n_("apk"))
        else:
            send(dst, T[LP][:], T[PK][:], [reg(PK)], reg(LP), n_("apk"))
        send(dst, u8(T[LQ][:]), u8(T[QX][:]), [reg(QX)], reg(LQ), n_("aq"))
        send(dst, T[LS][:], T[SX][:], [reg(SX)], reg(LS), n_("asc"))

        if r > 0:
            laid(r)
        else:
            quant("EQ", "ES", "ET")
            for b in range(4):
                mm(b, "EQ", "ES", 128 * b, QX, SX)
            op("V", lambda: v.tensor_scalar(T.FT0[:], T[PK][:, 0:20], 160.0, None, A.add), [reg(PK, 0, 20)], [reg("FT0")])
        for b in range(3):
            if r == 0:
                op("S", lambda: s.activation(T[F][:, C * b:C * b + C], T.PS[:, 512 * b:512 * b + C], COPY), [bank(b)], [reg(F, C * b, C * b + C)])
            else:
                op("V", lambda: v.tensor_copy(T[F][:, C * b:C * b + C], T.PS[:, 512 * b:512 * b + C]), [bank(b)], [reg(F, C * b, C * b + C)])
        if r == 0:
            op("V", lambda: v.tensor_copy(T.AI3[:].indirect(T.FT0[:]), T.IOS[:]), [reg("IOS"), reg("FT0")], [reg("AI3")])
        quant(QF, SF, XF)
        for b in range(4):
            mm(4 + b, "EQ", "ES", 128 * b, QF, SF, True, False)
        for b in range(4):
            mm(4 + b, "EQ", "ES", 128 * b, LQ, LS, False, True)
        if r == 0:
            gather_s(T[FS][:], reg(FS), T.IOS[:], reg("IOS"), T.FT0[:], reg("FT0"))
            op("V", lambda: v.tensor_tensor(T.MK[:], T.AI3[:], T.MSK[:], A.mult), [reg("AI3"), reg("MSK")], [reg("MK")])
            scan()
            sample(T[FI][:], reg(FI), 160.0)

        def tf(i):
            return T[TF][:, 20 * i:20 * i + 20]

        def rf(i):
            return reg(TF, 20 * i, 20 * i + 20)

        def tb(i):
            return T[TB][:, 20 * i:20 * i + 20]

        def rb(i):
            return reg(TB, 20 * i, 20 * i + 20)
        es, be, le, lb = T[LP][:, 0:20], T[LP][:, 20:40], reg(LP, 0, 20), reg(LP, 20, 40)
        op("V", lambda: v.tensor_tensor(tf(1), T.ATS[:], es, A.subtract), [le, reg("ATS")], [rf(1)])
        op("V", lambda: v.tensor_tensor(tf(0), be, T[PK][:, 20:40], A.not_equal), [lb, reg(PK, 20, 40)], [rf(0)])
        op("V", lambda: v.tensor_tensor(tf(2), tf(1), tf(0), A.mult), [rf(0), rf(1)], [rf(2)])
        op("V", lambda: v.tensor_scalar(tf(4), tf(0), -320.0, 480.0, A.mult, A.add), [rf(0)], [rf(4)])
        op("V", lambda: v.tensor_tensor(tf(3), tf(2), es, A.add), [rf(2), le], [rf(3)])
        op("V", lambda: v.tensor_tensor(tf(5), T.ATS[:], tf(2), A.subtract), [rf(2), reg("ATS")], [rf(5)])
        op("V", lambda: v.tensor_scalar(tb(0), tf(3), 160.0, None, A.add), [rf(3)], [rb(0)])

        def slot(k):
            return T[WN][:, C * k:C * k + C], reg(WN, C * k, C * k + C)
        H = C // 2

        def both(ob, lo, win, winreg, i):
            t = T[TB]
            op("V", lambda: v.tensor_copy(T[ob][:, lo:lo + H], win.indirect(t[:, 20 * i:20 * i + 10])), [winreg, rb(i)], [reg(ob, lo, lo + H)])
            op("S", lambda: s.activation(T[ob][:, lo + H:lo + C], win.indirect(t[:, 20 * i + 10:20 * i + 20]), COPY), [winreg, rb(i)], [reg(ob, lo + H, lo + C)])
            return T[ob][:, lo:lo + C], reg(ob, lo, lo + C)
        w = both(WN, 0, T.IOS[:], reg("IOS"), 0)
        op("V", lambda: v.tensor_tensor(tf(6), tf(5), tf(4), A.add), [rf(5), rf(4)], [rf(6)])

        def evac_m(b):
            op("S", lambda: s.activation(T[M][:, C * b:C * b + C], T.PS[:, 2048 + 512 * b:2048 + 512 * b + C], COPY), [bank(4 + b)], [reg(M, C * b, C * b + C)])
        nslot, cur, pt, pw = 1, 0, 1, 1
        for k, ahead in enumerate(STAGES):
            for i in range(ahead):
                w = both(WN, C * nslot, w[0], w[1], cur)
                nslot, pw = nslot + 1, pw + pt
            gather_masked(w[0], w[1], tb(cur), rb(cur))
            w2 = slot(nslot)
            gather_s(w2[0], w2[1], w[0], w[1], tb(cur), rb(cur))
            nslot += 1
            if k == 0:
                op("V", lambda: v.tensor_copy(tb(1), tf(6)), [rf(6)], [rb(1)])
            scan()
            cur, w = k + 2, w2
            pt, pw = pt + pw, pw + pt
            sample(tb(cur), rb(cur), 160.0)
            if k == len(STAGES) - 1:
                evac_m(0)
        for i in range(LAST):
            ob, lo = ("FW1", 0) if i == LAST - 1 else (WN, C * nslot)
            w = both(ob, lo, w[0], w[1], cur)
            pw += pt
        fin = len(STAGES) + 2
        gather_masked(T.FW1[:], reg("FW1"), tb(1), rb(1))
        gather_s(T.FW2[:, 0:C], reg("FW2", 0, C), w[0], w[1], tb(cur), rb(cur))
        scan()
        sample(tb(fin), rb(fin), 160.0)
        assert pw + (pw + pt) >= C - 1
        for b in range(1, 4):
            evac_m(b)
        gather_masked(T.FW2[:], reg("FW2"), tb(fin), rb(fin))
        scan()
        sample(T[AT][:], reg(AT), 160.0)

        def plane(name, b):
            return T[name][:, C * b:C * b + C], reg(name, C * b, C * b + C)
        mw, mr = plane(M, 0)
        op("V", lambda: v.tensor_copy(T[Z][:, 0:4 * C:4], mw.indirect(T[AT][:])), [mr, reg(AT)], [reg(Z, 0, 4 * C, 0)])
        for b in range(1, 4):
            mw, mr = plane(M, b)
            gather_s(T[Z][:, b:4 * C:4], reg(Z, 0, 4 * C, b), mw, mr, T[AT][:], reg(AT))
        op("V", lambda: v.tensor_copy(T[AI][:].indirect(T[AT][:]), T.IOS[:]), [reg("IOS"), reg(AT)], [reg(AI)])
        quant(QZ, SZ, Z)
        for b in range(4):
            mm(4 + b, "WQ", "WS", 128 * b, QZ, SZ)
        gather_s(T["FS" + nxt][:], reg("FS" + nxt), T[FS][:], reg(FS), T[AT][:], reg(AT))
        gather_masked(T[AI][:], reg(AI), T[FI][:], reg(FI))
        scan()
        sample(T["FI" + nxt][:], reg("FI" + nxt), 160.0)
        for b in range(4):
            op("S", lambda: s.activation(T[PW][:, C * b:C * b + C], T.PS[:, 2048 + 512 * b:2048 + 512 * b + C], COPY, scale=0.015625),
               [bank(4 + b)], [reg(PW, C * b, C * b + C)])
        fi, fir = T["FI" + nxt][:], reg("FI" + nxt)
        pw3, pr3 = plane(PW, 3)
        gather_s(T[B3][:], reg(B3), pw3, pr3, fi, fir)
        for b in range(3):
            pw_, pr = plane(PW, b)
            fw_, fr = plane(F, b)
            op("V", lambda: v.tensor_tensor(T["X" + nxt][:, b:4 * C:4], pw_.indirect(fi), fw_, A.add),
               [pr, fir, fr], [reg("X" + nxt, 0, 4 * C, b)])
        op("V", lambda: v.tensor_tensor(T["X" + nxt][:, 3:4 * C:4], T[B3][:], T.PS[:, 1536:1536 + C], A.add),
           [reg(B3), bank(3)], [reg("X" + nxt, 0, 4 * C, 3)])
        quant("QX" + nxt, "SX" + nxt, "X" + nxt)
        if r == 2:
            quant("VQ", "VS", "VT")

    mm(4, "VQ", "VS", 0, "QX3", "SX3")
    dma("Y", T.oc[:], u8(T.QX3[:]), [reg("QX3")], [])
    for k in range(4):
        dma("Y" if k % 2 else "S", T.osc[4 * k:4 * k + 4, :], T.SX3[32 * k:32 * k + 4, :], [reg("SX3")], [])
    op("V", lambda: v.tensor_scalar(T.LNF[:], T.FS3[:], 160.0, None, A.add), [reg("FS3")], [reg("LNF")])
    op("V", lambda: v.tensor_copy(T.YS[:], T.PS[:, 2048:2048 + C]), [bank(4)], [reg("YS")])
    dma("S", T.ln[:], T.LNF[0:128:16, :], [reg("LNF")], [])
    dma("Y", T.y[:], T.YS[:], [reg("YS")], [])
    for sem, val in count.items():
        g.wait_ge(T.sem[sem], val)
